import numpy as np
import ml_dtypes


def mxq(x, axis, fmt="e4m3"):
    dtype, down = {"e4m3": (ml_dtypes.float8_e4m3fn, 7), "e5m2": (ml_dtypes.float8_e5m2, 14)}[fmt]
    v = np.moveaxis(np.asarray(x, np.float32).astype(ml_dtypes.bfloat16).astype(np.float64), axis, -1)
    blocks = v.reshape(v.shape[:-1] + (-1, 32))
    amax = np.abs(blocks).max(-1, keepdims=True)
    byte = np.maximum(np.where(amax > 0, np.frexp(amax)[1] - 1 + 127, 0) - down, 1)
    scale = np.exp2(byte - 127.0)
    codes = (blocks / scale).astype(np.float32).astype(dtype).astype(np.float64)
    return np.moveaxis((codes * scale).reshape(v.shape), -1, axis)


WIDE = False


def mx_kscale(k):
    if not WIDE:
        return np.ones(k)
    levels = np.array([10, -10, 5, -5, 0])
    if k % 512:
        return np.exp2(np.random.permutation(np.resize(levels, k // 32))).repeat(32)
    a = np.empty((k // 512, 16))
    for p in range(k // 512):
        a[p, :8] = np.random.permutation(np.resize(levels, 8))
        for g in range(8):
            far = levels[np.abs(levels - a[p, g]) >= 10]
            a[p, g + 8] = far[np.random.randint(len(far))]
    return np.exp2(a.ravel()).repeat(32)


def f64(x):
    return np.asarray(x).astype(np.float64)


def striped(idx):
    return np.tile(idx.reshape(-1, 16).T, (8, 1)).astype(np.uint16)


def unstriped(offs):
    return offs[:16].T.reshape(-1).astype(np.int64)


E2M1 = np.array([0.0, 0.5, 1.0, 1.5, 2.0, 3.0, 4.0, 6.0, -0.0, -0.5, -1.0, -1.5, -2.0, -3.0, -4.0, -6.0])


def pack_weight(w, fmt):
    k, n = w.shape
    w = f64(np.asarray(w, np.float32).astype(ml_dtypes.bfloat16)).reshape(k // 32, 32, n)
    amax = np.abs(w).max(1)
    if fmt == "e4m3":
        byte = np.frexp(amax)[1] - 1 + 127 - 7
    else:
        mant, ex = np.frexp(amax / 6.0)
        byte = np.where(mant > 0.5, ex, ex - 1) + 127
    byte = np.clip(np.where(amax > 0, byte, 1), 1, 254)
    scaled = (w * np.exp2(127.0 - byte)[:, None, :]).reshape(k, n).astype(np.float32)
    by_word = np.ascontiguousarray(scaled.reshape(k // 512, 128, 4, n).transpose(0, 1, 3, 2))
    if fmt == "e4m3":
        words = by_word.astype(ml_dtypes.float8_e4m3fn).view(np.uint8)
    else:
        c = by_word.astype(ml_dtypes.float4_e2m1fn).view(np.uint8) & 0xF
        words = (c[..., 0::2] | (c[..., 1::2] << 4)).reshape(k // 512, 128, 2 * n)
    return np.ascontiguousarray(words), np.ascontiguousarray(byte.astype(np.uint8).reshape(k // 512, 16, n))


def unpack_weight(words, scales, fmt):
    g, _, n = scales.shape
    words = np.ascontiguousarray(words).reshape(g, 128, n, -1)
    if fmt == "e4m3":
        vals = words.view(ml_dtypes.float8_e4m3fn).astype(np.float64)
    else:
        nib = np.empty((g, 128, n, 4), np.uint8)
        nib[..., 0::2] = words & 0xF
        nib[..., 1::2] = words >> 4
        vals = E2M1[nib]
    vals = vals * np.repeat(np.exp2(scales.astype(np.float64) - 127.0), 8, axis=1)[..., None]
    return vals.transpose(0, 1, 3, 2).reshape(g * 512, n)


def gelu(v):
    return 0.5 * v * (1.0 + np.tanh(np.sqrt(2.0 / np.pi) * (v + 0.044715 * v**3)))


K, T, E, C, H, N = 1536, 640, 2, 256, 1024, 384


def by_expert(wq, xq):
    return np.concatenate([wq[e].T @ xq[:, e * C:(e + 1) * C] for e in range(E)], axis=1)


def setup_inputs():
    n = np.random.standard_normal
    s = mx_kscale(K)[:, None]
    u = mx_kscale(H)
    w1 = [pack_weight(m, "e2m1") for m in n((E, K, H)) / np.sqrt(K) / s[None] * u[None, None, :]]
    w2 = [pack_weight(m, "e2m1") for m in n((E, H, N)) / np.sqrt(H) / u[None, :, None]]
    return {
        "xT": (n((K, T)) * s).astype(np.float32),
        "xr": n((N, T)).astype(np.float32),
        "w1_words": np.stack([m[0] for m in w1]),
        "w1_scales": np.stack([m[1] for m in w1]),
        "w2_words": np.stack([m[0] for m in w2]),
        "w2_scales": np.stack([m[1] for m in w2]),
        "gate": np.tile(np.random.uniform(0.2, 1.0, E * C), (N, 1)).astype(np.float32),
        "offs": striped(np.random.permutation(T)[:E * C]),
    }


def reference(xT, xr, w1_words, w1_scales, w2_words, w2_scales, gate, offs):
    idx = unstriped(offs)
    w1 = np.stack([unpack_weight(w1_words[e], w1_scales[e], "e2m1") for e in range(E)])
    w2 = np.stack([unpack_weight(w2_words[e], w2_scales[e], "e2m1") for e in range(E)])
    xq = mxq(f64(xT)[:, idx], 0, "e4m3")
    h = gelu(by_expert(w1, xq))
    y = by_expert(w2, mxq(h, 0, "e4m3"))
    out = f64(xr).copy()
    out[:, idx] += f64(gate) * y
    return out

@@ -1,0 +1,259 @@
+from contextlib import ExitStack
+
+import concourse.mybir as mybir
+from concourse.masks import make_identity
+
+K, T, E, C, H, N = 1536, 640, 2, 256, 1024, 384
+P = 128
+FLOPS = 2 * E * C * (K * H + H * N)
+
+F32 = mybir.dt.float32
+BF16 = mybir.dt.bfloat16
+I32 = mybir.dt.int32
+U32 = mybir.dt.uint32
+U16 = mybir.dt.uint16
+U8 = mybir.dt.uint8
+FP8X4 = mybir.dt.float8_e4m3fn_x4
+FP4X4 = mybir.dt.float4_e2m1fn_x4
+ACT = mybir.ActivationFunctionType
+MULT = mybir.AluOpType.mult
+
+KP = K // 512
+HP = H // 512
+NB = N // P
+S = E * C // P
+
+
+def tile_moe_res_mlp_gelu_kernel(
+    tc, xT, xr, w1_words, w1_scales, w2_words, w2_scales, gate, offs, out
+):
+    nc = tc.nc
+    with ExitStack() as ctx:
+        keep = ctx.enter_context(tc.tile_pool(name="keep", bufs=1))
+        mmp = ctx.enter_context(tc.psum_pool(name="mmp", bufs=4))
+        xtp = ctx.enter_context(tc.psum_pool(name="xtp", bufs=2))
+        yp = ctx.enter_context(tc.psum_pool(name="yp", bufs=2))
+
+        offsets = keep.tile([P, E * C // 16], U16, name="offsets")
+
+        x_raw = [keep.tile([P, 4, T], F32, name="x_raw%d" % s) for s in range(KP)]
+        x_bf = [keep.tile([P, T, 4], BF16, align_bytes=64, name="x_bf%d" % s) for s in range(KP)]
+        x_words = [keep.tile([P, T], U32, align_bytes=64, name="x_words%d" % s) for s in range(KP)]
+        x_bytes = [keep.tile([P, T], U8, align_bytes=64, name="x_bytes%d" % s) for s in range(KP)]
+        g_words = [[keep.tile([P, C], U32, align_bytes=64, name="g_words%d_%d" % (s, e)) for e in range(E)] for s in range(KP)]
+        g_bytes = [[keep.tile([P, C], U8, align_bytes=64, name="g_bytes%d_%d" % (s, e)) for e in range(E)] for s in range(KP)]
+        w1_t = [[keep.tile([P, 2 * H], U8, align_bytes=64, name="w1_%d_%d" % (e, s)) for s in range(KP)] for e in range(E)]
+        w1_s = [keep.tile([P, KP * H], U8, align_bytes=64, name="w1s_%d" % e) for e in range(E)]
+        w2_t = [keep.tile([P, HP * 2 * N], U8, align_bytes=64, name="w2_%d" % e) for e in range(E)]
+        w2_s = keep.tile([P, E * HP * N], U8, align_bytes=64, name="w2s")
+        gate_t = keep.tile([P, NB, E * C], F32, name="gate_t")
+        xr_t = [keep.tile([P, T], F32, name="xr_%d" % m) for m in range(NB)]
+        win = [keep.tile([P, T], F32, name="win_%d" % m) for m in range(NB)]
+        res = [keep.tile([P, T], F32, name="res_%d" % m) for m in range(NB)]
+        h_bf = [keep.tile([P, H], BF16, align_bytes=64, name="h_bf%d" % s) for s in range(S)]
+        h_gr = [keep.tile([P, HP, P, 4], BF16, align_bytes=64, name="h_gr%d" % s) for s in range(S)]
+        h_words = [keep.tile([P, HP * P], U32, align_bytes=64, name="h_words%d" % s) for s in range(S)]
+        h_bytes = [keep.tile([P, HP * P], U8, align_bytes=64, name="h_bytes%d" % s) for s in range(S)]
+        y_g = [keep.tile([P, NB, P], F32, name="y_g%d" % s) for s in range(S)]
+        ident = keep.tile([P, P], F32, name="ident")
+        warm = keep.tile([P, 1], F32, name="warm")
+
+        nc.vector.memset(warm[:], 0.0)
+        nc.scalar.activation(warm[:], warm[:], ACT.Gelu_apprx_tanh)
+        for e in range(E):
+            nc.vector.memset(w1_s[e][:].bitcast(I32), 0)
+        nc.vector.memset(w2_s[:].bitcast(I32), 0)
+        for s in range(KP):
+            nc.gpsimd.memset(x_bytes[s][:].bitcast(I32), 0)
+        make_identity(nc, ident[:])
+        for m in range(NB):
+            nc.gpsimd.memset(win[m][:], 0.0)
+
+        def load_x(s, c0, c1):
+            nc.sync.dma_start(
+                x_raw[s][:, :, c0:c1],
+                xT[512 * s : 512 * (s + 1), :].rearrange("(p j) w -> p j w", j=4)[:, :, c0:c1],
+            )
+
+        def load_w1(e, s):
+            nc.sync.dma_start(w1_t[e][s][:].bitcast(I32), w1_words[e, s].bitcast(I32))
+
+        def load_scales1(e):
+            planes = w1_s[e][:].bitcast(I32).rearrange("p (s c) -> p s c", s=KP)
+            rows = w1_scales[e].bitcast(I32).rearrange("s (q r) c -> r q s c", r=4)
+            for r in range(4):
+                nc.sync.dma_start(planes[r:P:32], rows[r])
+
+        load_x(0, 0, 256)
+        load_x(0, 256, T)
+        nc.sync.dma_start(offsets[:], offs)
+        load_x(1, 0, 384)
+        load_x(1, 384, T)
+        load_scales1(0)
+        load_w1(0, 0)
+        load_x(2, 0, 384)
+        load_x(2, 384, T)
+        load_w1(0, 1)
+        load_w1(0, 2)
+        planes2 = w2_s[:].bitcast(I32).rearrange("p (g c) -> p g c", g=E * HP)
+        rows2 = w2_scales.bitcast(I32).rearrange("e g (q r) c -> r q (e g) c", r=4)
+        for r in range(4):
+            nc.sync.dma_start(planes2[r:P:32], rows2[r])
+        load_scales1(1)
+        for e in range(E):
+            nc.sync.dma_start(
+                w2_t[e][:].bitcast(I32).rearrange("p (g c) -> p g c", g=HP),
+                w2_words[e].bitcast(I32).rearrange("g p c -> p g c"),
+            )
+        nc.sync.dma_start(gate_t[:], gate.rearrange("(m p) c -> p m c", p=P))
+        for s in range(KP):
+            load_w1(1, s)
+        for m in range(NB):
+            nc.sync.dma_start(xr_t[m][:], xr[m * P : (m + 1) * P, :])
+
+        def cast(eng, s, c0, c1):
+            dst = x_bf[s][:, c0:c1, :].rearrange("p (c i) t -> p c t i", i=4)
+            source = x_raw[s][:, :, c0:c1].rearrange("p t (c i) -> p c t i", i=4)
+            if eng == "v":
+                nc.vector.tensor_copy(dst, source)
+            else:
+                nc.scalar.activation(dst, source, ACT.Copy)
+
+        def quant_x(s, c0, c1):
+            nc.vector.quantize_mx(
+                out=x_words[s][:, c0:c1].bitcast(FP8X4),
+                scales=x_bytes[s][:, c0:c1],
+                in_=x_bf[s][:, c0:c1, :].rearrange("p c t -> p (c t)"),
+            )
+
+        def gather(s, e):
+            idx = offsets[:, e * (C // 16) : (e + 1) * (C // 16)]
+            nc.vector.tensor_copy(g_words[s][e][:], x_words[s][:].indirect(idx))
+            nc.vector.tensor_copy(g_bytes[s][e][:], x_bytes[s][:].indirect(idx))
+
+        banks = {}
+
+        def mm1(t, s):
+            e, c0 = t // 2, (t % 2) * P
+            for b in range(HP):
+                if s == 0:
+                    banks[t, b] = mmp.tile([P, 512], F32, name="acc")
+                nc.tensor.matmul_mx(
+                    out=banks[t, b][:],
+                    lhsT=g_words[s][e][:, c0 : c0 + P].bitcast(FP8X4),
+                    lhsT_scale=g_bytes[s][e][:, c0 : c0 + P],
+                    rhs=w1_t[e][s][:, b * 1024 : (b + 1) * 1024].bitcast(FP4X4),
+                    rhs_scale=w1_s[e][:, s * H + b * 512 : s * H + (b + 1) * 512],
+                    start=(s == 0),
+                    stop=(s == KP - 1),
+                )
+
+        def gelu(t):
+            for b in range(HP):
+                nc.scalar.activation(
+                    h_bf[t][:, b * 512 : (b + 1) * 512].rearrange("c (u p e) -> c u p e", u=2, e=2),
+                    banks[t, b][:].rearrange("c (p u e) -> c u p e", u=2, e=2),
+                    ACT.Gelu_apprx_tanh,
+                )
+
+        def turn(t):
+            xt = xtp.tile([P, HP, 2, P], F32, name="xt")
+            pairs = h_bf[t][:].bitcast(F32)
+            for b in range(HP):
+                for u in range(2):
+                    nc.tensor.transpose(xt[:, b, u, :], pairs[:, b * 256 + u * P : b * 256 + (u + 1) * P], ident[:])
+            nc.scalar.copy(
+                h_gr[t][:].rearrange("p b c t -> p (b c t)").bitcast(F32).rearrange("p (b c u) -> p b c u", b=HP, u=2),
+                xt[:].rearrange("p b u c -> p b c u"),
+            )
+
+        def quant_h(t):
+            nc.vector.quantize_mx(
+                out=h_words[t][:].bitcast(FP8X4),
+                scales=h_bytes[t][:],
+                in_=h_gr[t][:].rearrange("p b c t -> p (b c t)"),
+            )
+
+        def mm2(t):
+            e = t // 2
+            y = yp.tile([P, NB, P], F32, name="y")
+            for m in range(NB):
+                for b in range(HP):
+                    w0 = b * N + m * P
+                    nc.tensor.matmul_mx(
+                        out=y[:, m, :],
+                        lhsT=w2_t[e][:, 2 * w0 : 2 * (w0 + P)].bitcast(FP4X4),
+                        lhsT_scale=w2_s[:, e * HP * N + w0 : e * HP * N + w0 + P],
+                        rhs=h_words[t][:, b * P : (b + 1) * P].bitcast(FP8X4),
+                        rhs_scale=h_bytes[t][:, b * P : (b + 1) * P],
+                        start=(b == 0),
+                        stop=(b == HP - 1),
+                    )
+            nc.scalar.copy(y_g[t][:], y[:])
+
+        def scatter(t):
+            idx = offsets[:, t * (P // 16) : (t + 1) * (P // 16)]
+            for m in range(NB):
+                nc.vector.tensor_tensor(win[m][:].indirect(idx), y_g[t][:, m, :], gate_t[:, m, t * P : (t + 1) * P], MULT)
+
+        cast("s", 0, 0, 128)
+        cast("v", 0, 128, 256)
+        quant_x(0, 0, 256)
+        cast("s", 0, 256, 512)
+        cast("v", 0, 512, T)
+        quant_x(0, 512, T)
+        quant_x(0, 256, 512)
+        gather(0, 0)
+        mm1(0, 0)
+        mm1(1, 0)
+        gather(0, 1)
+        cast("s", 1, 0, 256)
+        cast("v", 1, 256, 384)
+        quant_x(1, 256, 384)
+        quant_x(1, 0, 256)
+        cast("s", 1, 384, T)
+        quant_x(1, 384, T)
+        gather(1, 0)
+        mm1(0, 1)
+        mm1(1, 1)
+        cast("s", 2, 0, 256)
+        quant_x(2, 0, 256)
+        cast("s", 2, 256, 384)
+        quant_x(2, 256, 384)
+        cast("s", 2, 384, 512)
+        cast("v", 2, 512, T)
+        quant_x(2, 384, T)
+        gather(2, 0)
+        mm1(0, 2)
+        mm1(1, 2)
+        gelu(0)
+        gather(1, 1)
+        gather(2, 1)
+        turn(0)
+        gelu(1)
+        quant_h(0)
+        for s in range(KP):
+            mm1(2, s)
+        mm2(0)
+        turn(1)
+        gelu(2)
+        scatter(0)
+        quant_h(1)
+        for s in range(KP):
+            mm1(3, s)
+        mm2(1)
+        turn(2)
+        gelu(3)
+        scatter(1)
+        quant_h(2)
+        mm2(2)
+        turn(3)
+        scatter(2)
+        quant_h(3)
+        mm2(3)
+        idx = offsets[:, 3 * (P // 16) : 4 * (P // 16)]
+        for m in range(NB):
+            nc.vector.tensor_tensor(win[m][:].indirect(idx), y_g[3][:, m, :], gate_t[:, m, 3 * P : 4 * P], MULT)
+            eng = nc.vector if m == NB - 1 else nc.gpsimd
+            eng.tensor_tensor(res[m][:], win[m][:], xr_t[m][:], mybir.AluOpType.add)
+            nc.sync.dma_start(out[m * P : (m + 1) * P, :], res[m][:])

@@ -189,12 +189,12 @@ def tile_moe_res_mlp_gelu_kernel(
                         start=(b == 0),
                         stop=(b == HP - 1),
                     )
-            nc.scalar.copy(y_g[t][:], y[:])
+            nc.vector.tensor_tensor(y_g[t][:], y[:], gate_t[:, :, t * P : (t + 1) * P], MULT)
 
         def scatter(t):
             idx = offsets[:, t * (P // 16) : (t + 1) * (P // 16)]
             for m in range(NB):
-                nc.vector.tensor_tensor(win[m][:].indirect(idx), y_g[t][:, m, :], gate_t[:, m, t * P : (t + 1) * P], MULT)
+                nc.vector.tensor_copy(win[m][:].indirect(idx), y_g[t][:, m, :])
 
         cast("s", 0, 0, 128)
         cast("v", 0, 128, 256)
@@ -253,7 +253,7 @@ def tile_moe_res_mlp_gelu_kernel(
         mm2(3)
         idx = offsets[:, 3 * (P // 16) : 4 * (P // 16)]
         for m in range(NB):
-            nc.vector.tensor_tensor(win[m][:].indirect(idx), y_g[3][:, m, :], gate_t[:, m, 3 * P : 4 * P], MULT)
+            nc.vector.tensor_copy(win[m][:].indirect(idx), y_g[3][:, m, :])
             eng = nc.vector if m == NB - 1 else nc.gpsimd
             eng.tensor_tensor(res[m][:], win[m][:], xr_t[m][:], mybir.AluOpType.add)
             nc.sync.dma_start(out[m * P : (m + 1) * P, :], res[m][:])

@@ -36,12 +36,11 @@ def tile_moe_res_mlp_gelu_kernel(
 
         offsets = keep.tile([P, E * C // 16], U16, name="offsets")
 
-        x_raw = [keep.tile([P, 4, T], F32, name="x_raw%d" % s) for s in range(KP)]
-        x_bf = [keep.tile([P, T, 4], BF16, align_bytes=64, name="x_bf%d" % s) for s in range(KP)]
+        x_raw = [keep.tile([P, 4, T], F32, align_bytes=64, name="x_raw%d" % s, tag="x_raw%d" % s) for s in range(KP)]
+        x_bf = [keep.tile([P, T, 4], BF16, align_bytes=64, name="x_bf%d" % s, tag="x_bf%d" % s) for s in range(KP)]
         x_words = [keep.tile([P, T], U32, align_bytes=64, name="x_words%d" % s) for s in range(KP)]
         x_bytes = [keep.tile([P, T], U8, align_bytes=64, name="x_bytes%d" % s) for s in range(KP)]
-        g_words = [[keep.tile([P, C], U32, align_bytes=64, name="g_words%d_%d" % (s, e)) for e in range(E)] for s in range(KP)]
-        g_bytes = [[keep.tile([P, C], U8, align_bytes=64, name="g_bytes%d_%d" % (s, e)) for e in range(E)] for s in range(KP)]
+        g_words, g_bytes = {}, {}
         w1_t = [[keep.tile([P, 2 * H], U8, align_bytes=64, name="w1_%d_%d" % (e, s)) for s in range(KP)] for e in range(E)]
         w1_s = [keep.tile([P, KP * H], U8, align_bytes=64, name="w1s_%d" % e) for e in range(E)]
         w2_t = [keep.tile([P, HP * 2 * N], U8, align_bytes=64, name="w2_%d" % e) for e in range(E)]
@@ -84,15 +83,16 @@ def tile_moe_res_mlp_gelu_kernel(
             for r in range(4):
                 nc.sync.dma_start(planes[r:P:32], rows[r])
 
-        load_x(0, 0, 256)
-        load_x(0, 256, T)
+        CHUNKS = ((0, 256), (256, 512), (512, T))
+        for c in CHUNKS:
+            load_x(0, *c)
         nc.sync.dma_start(offsets[:], offs)
-        load_x(1, 0, 384)
-        load_x(1, 384, T)
+        for c in CHUNKS:
+            load_x(1, *c)
         load_scales1(0)
         load_w1(0, 0)
-        load_x(2, 0, 384)
-        load_x(2, 384, T)
+        for c in CHUNKS:
+            load_x(2, *c)
         load_w1(0, 1)
         load_w1(0, 2)
         planes2 = w2_s[:].bitcast(I32).rearrange("p (g c) -> p g c", g=E * HP)
@@ -105,9 +105,9 @@ def tile_moe_res_mlp_gelu_kernel(
                 w2_t[e][:].bitcast(I32).rearrange("p (g c) -> p g c", g=HP),
                 w2_words[e].bitcast(I32).rearrange("g p c -> p g c"),
             )
-        nc.sync.dma_start(gate_t[:], gate.rearrange("(m p) c -> p m c", p=P))
         for s in range(KP):
             load_w1(1, s)
+        nc.sync.dma_start(gate_t[:], gate.rearrange("(m p) c -> p m c", p=P))
         for m in range(NB):
             nc.sync.dma_start(xr_t[m][:], xr[m * P : (m + 1) * P, :])
 
@@ -126,10 +126,22 @@ def tile_moe_res_mlp_gelu_kernel(
                 in_=x_bf[s][:, c0:c1, :].rearrange("p c t -> p (c t)"),
             )
 
-        def gather(s, e):
-            idx = offsets[:, e * (C // 16) : (e + 1) * (C // 16)]
-            nc.vector.tensor_copy(g_words[s][e][:], x_words[s][:].indirect(idx))
-            nc.vector.tensor_copy(g_bytes[s][e][:], x_bytes[s][:].indirect(idx))
+        def tokens(s):
+            cast("s", s, 0, 256)
+            cast("s", s, 256, 384)
+            cast("v", s, 384, 512)
+            cast("s", s, 512, T)
+            for c in CHUNKS:
+                quant_x(s, *c)
+
+        def gather_tiles(s, e, words_tag, bytes_tag):
+            g_words[s, e] = keep.tile([P, C], U32, align_bytes=64, name="g_words%d_%d" % (s, e), tag=words_tag)
+            g_bytes[s, e] = keep.tile([P, C], U8, align_bytes=64, name="g_bytes%d_%d" % (s, e), tag=bytes_tag)
+
+        def gather(s, e, c0, c1):
+            idx = offsets[:, (e * C + c0) // 16 : (e * C + c1) // 16]
+            nc.vector.tensor_copy(g_words[s, e][:, c0:c1], x_words[s][:].indirect(idx))
+            nc.vector.tensor_copy(g_bytes[s, e][:, c0:c1], x_bytes[s][:].indirect(idx))
 
         banks = {}
 
@@ -140,34 +152,31 @@ def tile_moe_res_mlp_gelu_kernel(
                     banks[t, b] = mmp.tile([P, 512], F32, name="acc")
                 nc.tensor.matmul_mx(
                     out=banks[t, b][:],
-                    lhsT=g_words[s][e][:, c0 : c0 + P].bitcast(FP8X4),
-                    lhsT_scale=g_bytes[s][e][:, c0 : c0 + P],
+                    lhsT=g_words[s, e][:, c0 : c0 + P].bitcast(FP8X4),
+                    lhsT_scale=g_bytes[s, e][:, c0 : c0 + P],
                     rhs=w1_t[e][s][:, b * 1024 : (b + 1) * 1024].bitcast(FP4X4),
                     rhs_scale=w1_s[e][:, s * H + b * 512 : s * H + (b + 1) * 512],
                     start=(s == 0),
                     stop=(s == KP - 1),
                 )
 
-        def gelu(t):
+        def hidden(t, engs="ss"):
             for b in range(HP):
                 nc.scalar.activation(
                     h_bf[t][:, b * 512 : (b + 1) * 512].rearrange("c (u p e) -> c u p e", u=2, e=2),
                     banks[t, b][:].rearrange("c (p u e) -> c u p e", u=2, e=2),
                     ACT.Gelu_apprx_tanh,
                 )
-
-        def turn(t):
-            xt = xtp.tile([P, HP, 2, P], F32, name="xt")
-            pairs = h_bf[t][:].bitcast(F32)
-            for b in range(HP):
+                xt = xtp.tile([P, 2, P], F32, name="xt")
+                pairs = h_bf[t][:].bitcast(F32)
                 for u in range(2):
-                    nc.tensor.transpose(xt[:, b, u, :], pairs[:, b * 256 + u * P : b * 256 + (u + 1) * P], ident[:])
-            nc.scalar.copy(
-                h_gr[t][:].rearrange("p b c t -> p (b c t)").bitcast(F32).rearrange("p (b c u) -> p b c u", b=HP, u=2),
-                xt[:].rearrange("p b u c -> p b c u"),
-            )
-
-        def quant_h(t):
+                    nc.tensor.transpose(xt[:, u, :], pairs[:, b * 256 + u * P : b * 256 + (u + 1) * P], ident[:])
+                dst = h_gr[t][:, b].rearrange("p c t -> p (c t)").bitcast(F32).rearrange("p (c u) -> p c u", u=2)
+                source = xt[:].rearrange("p u c -> p c u")
+                if engs[b] == "s":
+                    nc.scalar.copy(dst, source)
+                else:
+                    nc.vector.tensor_copy(dst, source)
             nc.vector.quantize_mx(
                 out=h_words[t][:].bitcast(FP8X4),
                 scales=h_bytes[t][:],
@@ -189,71 +198,57 @@ def tile_moe_res_mlp_gelu_kernel(
                         start=(b == 0),
                         stop=(b == HP - 1),
                     )
-            nc.vector.tensor_tensor(y_g[t][:], y[:], gate_t[:, :, t * P : (t + 1) * P], MULT)
+            nc.scalar.copy(y_g[t][:], y[:])
 
-        def scatter(t):
+        def scatter(t, m):
             idx = offsets[:, t * (P // 16) : (t + 1) * (P // 16)]
-            for m in range(NB):
-                nc.vector.tensor_copy(win[m][:].indirect(idx), y_g[t][:, m, :])
+            nc.vector.tensor_tensor(win[m][:].indirect(idx), y_g[t][:, m, :], gate_t[:, m, t * P : (t + 1) * P], MULT)
 
-        cast("s", 0, 0, 128)
-        cast("v", 0, 128, 256)
-        quant_x(0, 0, 256)
-        cast("s", 0, 256, 512)
-        cast("v", 0, 512, T)
-        quant_x(0, 512, T)
-        quant_x(0, 256, 512)
-        gather(0, 0)
+        def finish(m):
+            nc.vector.tensor_tensor(res[m][:], win[m][:], xr_t[m][:], mybir.AluOpType.add)
+            nc.sync.dma_start(out[m * P : (m + 1) * P, :], res[m][:])
+
+        for s in range(KP):
+            gather_tiles(s, 0, "g_words%d_0" % s, "g_bytes%d_0" % s)
+        gather_tiles(0, 1, "g_words0_1", "g_bytes0_1")
+        gather_tiles(2, 1, "g_words2_1", "g_bytes2_1")
+        tokens(0)
+        gather(0, 0, 0, C)
         mm1(0, 0)
         mm1(1, 0)
-        gather(0, 1)
-        cast("s", 1, 0, 256)
-        cast("v", 1, 256, 384)
-        quant_x(1, 256, 384)
-        quant_x(1, 0, 256)
-        cast("s", 1, 384, T)
-        quant_x(1, 384, T)
-        gather(1, 0)
+        gather(0, 1, 0, C)
+        tokens(1)
+        gather(1, 0, 0, C)
         mm1(0, 1)
         mm1(1, 1)
-        cast("s", 2, 0, 256)
-        quant_x(2, 0, 256)
-        cast("s", 2, 256, 384)
-        quant_x(2, 256, 384)
-        cast("s", 2, 384, 512)
-        cast("v", 2, 512, T)
-        quant_x(2, 384, T)
-        gather(2, 0)
-        mm1(0, 2)
-        mm1(1, 2)
-        gelu(0)
-        gather(1, 1)
-        gather(2, 1)
-        turn(0)
-        gelu(1)
-        quant_h(0)
+        tokens(2)
+        for t in range(2):
+            gather(2, 0, t * P, (t + 1) * P)
+            mm1(t, 2)
+        hidden(0, "sv")
+        mm2(0)
+        gather_tiles(1, 1, "x_bf2", "x_raw2")
+        gather(1, 1, 0, C)
+        gather(2, 1, 0, C)
+        hidden(1)
+        mm2(1)
         for s in range(KP):
             mm1(2, s)
-        mm2(0)
-        turn(1)
-        gelu(2)
-        scatter(0)
-        quant_h(1)
+        for m in range(NB):
+            scatter(0, m)
+        hidden(2)
+        mm2(2)
         for s in range(KP):
             mm1(3, s)
-        mm2(1)
-        turn(2)
-        gelu(3)
-        scatter(1)
-        quant_h(2)
-        mm2(2)
-        turn(3)
-        scatter(2)
-        quant_h(3)
-        mm2(3)
-        idx = offsets[:, 3 * (P // 16) : 4 * (P // 16)]
         for m in range(NB):
-            nc.vector.tensor_copy(win[m][:].indirect(idx), y_g[3][:, m, :])
-            eng = nc.vector if m == NB - 1 else nc.gpsimd
-            eng.tensor_tensor(res[m][:], win[m][:], xr_t[m][:], mybir.AluOpType.add)
-            nc.sync.dma_start(out[m * P : (m + 1) * P, :], res[m][:])
+            scatter(1, m)
+        hidden(3)
+        mm2(3)
+        for m in range(NB):
+            scatter(2, m)
+        scatter(3, 0)
+        scatter(3, 1)
+        finish(0)
+        scatter(3, 2)
+        finish(1)
+        finish(2)

@@ -84,11 +84,10 @@ def tile_moe_res_mlp_gelu_kernel(
                 nc.sync.dma_start(planes[r:P:32], rows[r])
 
         CHUNKS = ((0, 256), (256, 512), (512, T))
-        for c in CHUNKS:
-            load_x(0, *c)
+        load_x(0, 0, 256)
+        load_x(0, 256, T)
         nc.sync.dma_start(offsets[:], offs)
-        for c in CHUNKS:
-            load_x(1, *c)
+        load_x(1, 0, T)
         load_scales1(0)
         load_w1(0, 0)
         for c in CHUNKS:
@@ -214,13 +213,12 @@ def tile_moe_res_mlp_gelu_kernel(
         gather_tiles(2, 1, "g_words2_1", "g_bytes2_1")
         tokens(0)
         gather(0, 0, 0, C)
-        mm1(0, 0)
-        mm1(1, 0)
         gather(0, 1, 0, C)
         tokens(1)
         gather(1, 0, 0, C)
-        mm1(0, 1)
-        mm1(1, 1)
+        for t in range(2):
+            mm1(t, 0)
+            mm1(t, 1)
         tokens(2)
         for t in range(2):
             gather(2, 0, t * P, (t + 1) * P)

from contextlib import ExitStack

import concourse.mybir as mybir
from concourse.masks import make_identity

K, T, E, C, H, N = 1536, 640, 2, 256, 1024, 384
P = 128
FLOPS = 2 * E * C * (K * H + H * N)

F32 = mybir.dt.float32
BF16 = mybir.dt.bfloat16
I32 = mybir.dt.int32
U32 = mybir.dt.uint32
U16 = mybir.dt.uint16
U8 = mybir.dt.uint8
FP8X4 = mybir.dt.float8_e4m3fn_x4
FP4X4 = mybir.dt.float4_e2m1fn_x4
ACT = mybir.ActivationFunctionType
MULT = mybir.AluOpType.mult

KP = K // 512
HP = H // 512
NB = N // P
S = E * C // P


def tile_moe_res_mlp_gelu_kernel(
    tc, xT, xr, w1_words, w1_scales, w2_words, w2_scales, gate, offs, out
):
    nc = tc.nc
    with ExitStack() as ctx:
        keep = ctx.enter_context(tc.tile_pool(name="keep", bufs=1))
        mmp = ctx.enter_context(tc.psum_pool(name="mmp", bufs=4))
        xtp = ctx.enter_context(tc.psum_pool(name="xtp", bufs=2))
        yp = ctx.enter_context(tc.psum_pool(name="yp", bufs=2))

        offsets = keep.tile([P, E * C // 16], U16, name="offsets")

        x_raw = [keep.tile([P, 4, T], F32, align_bytes=64, name="x_raw%d" % s, tag="x_raw%d" % s) for s in range(KP)]
        x_bf = [keep.tile([P, T, 4], BF16, align_bytes=64, name="x_bf%d" % s, tag="x_bf%d" % s) for s in range(KP)]
        x_words = [keep.tile([P, T], U32, align_bytes=64, name="x_words%d" % s) for s in range(KP)]
        x_bytes = [keep.tile([P, T], U8, align_bytes=64, name="x_bytes%d" % s) for s in range(KP)]
        g_words, g_bytes = {}, {}
        w1_t = [[keep.tile([P, 2 * H], U8, align_bytes=64, name="w1_%d_%d" % (e, s)) for s in range(KP)] for e in range(E)]
        w1_s = [keep.tile([P, KP * H], U8, align_bytes=64, name="w1s_%d" % e) for e in range(E)]
        w2_t = [keep.tile([P, HP * 2 * N], U8, align_bytes=64, name="w2_%d" % e) for e in range(E)]
        w2_s = keep.tile([P, E * HP * N], U8, align_bytes=64, name="w2s")
        gate_t = keep.tile([P, NB, E * C], F32, name="gate_t")
        xr_t = [keep.tile([P, T], F32, name="xr_%d" % m) for m in range(NB)]
        win = [keep.tile([P, T], F32, name="win_%d" % m) for m in range(NB)]
        res = [keep.tile([P, T], F32, name="res_%d" % m) for m in range(NB)]
        h_bf = [keep.tile([P, H], BF16, align_bytes=64, name="h_bf%d" % s) for s in range(S)]
        h_gr = [keep.tile([P, HP, P, 4], BF16, align_bytes=64, name="h_gr%d" % s) for s in range(S)]
        h_words = [keep.tile([P, HP * P], U32, align_bytes=64, name="h_words%d" % s) for s in range(S)]
        h_bytes = [keep.tile([P, HP * P], U8, align_bytes=64, name="h_bytes%d" % s) for s in range(S)]
        y_g = [keep.tile([P, NB, P], F32, name="y_g%d" % s) for s in range(S)]
        ident = keep.tile([P, P], F32, name="ident")
        warm = keep.tile([P, 1], F32, name="warm")

        nc.vector.memset(warm[:], 0.0)
        nc.scalar.activation(warm[:], warm[:], ACT.Gelu_apprx_tanh)
        for e in range(E):
            nc.vector.memset(w1_s[e][:].bitcast(I32), 0)
        nc.vector.memset(w2_s[:].bitcast(I32), 0)
        for s in range(KP):
            nc.gpsimd.memset(x_bytes[s][:].bitcast(I32), 0)
        make_identity(nc, ident[:])
        for m in range(NB):
            nc.gpsimd.memset(win[m][:], 0.0)

        def load_x(s, c0, c1):
            nc.sync.dma_start(
                x_raw[s][:, :, c0:c1],
                xT[512 * s : 512 * (s + 1), :].rearrange("(p j) w -> p j w", j=4)[:, :, c0:c1],
            )

        def load_w1(e, s):
            nc.sync.dma_start(w1_t[e][s][:].bitcast(I32), w1_words[e, s].bitcast(I32))

        def load_scales1(e):
            planes = w1_s[e][:].bitcast(I32).rearrange("p (s c) -> p s c", s=KP)
            rows = w1_scales[e].bitcast(I32).rearrange("s (q r) c -> r q s c", r=4)
            for r in range(4):
                nc.sync.dma_start(planes[r:P:32], rows[r])

        CHUNKS = ((0, 256), (256, 512), (512, T))
        load_x(0, 0, 256)
        load_x(0, 256, T)
        nc.sync.dma_start(offsets[:], offs)
        load_x(1, 0, T)
        load_scales1(0)
        load_w1(0, 0)
        for c in CHUNKS:
            load_x(2, *c)
        load_w1(0, 1)
        load_w1(0, 2)
        planes2 = w2_s[:].bitcast(I32).rearrange("p (g c) -> p g c", g=E * HP)
        rows2 = w2_scales.bitcast(I32).rearrange("e g (q r) c -> r q (e g) c", r=4)
        for r in range(4):
            nc.sync.dma_start(planes2[r:P:32], rows2[r])
        load_scales1(1)
        for e in range(E):
            nc.sync.dma_start(
                w2_t[e][:].bitcast(I32).rearrange("p (g c) -> p g c", g=HP),
                w2_words[e].bitcast(I32).rearrange("g p c -> p g c"),
            )
        for s in range(KP):
            load_w1(1, s)
        nc.sync.dma_start(gate_t[:], gate.rearrange("(m p) c -> p m c", p=P))
        for m in range(NB):
            nc.sync.dma_start(xr_t[m][:], xr[m * P : (m + 1) * P, :])

        def cast(eng, s, c0, c1):
            dst = x_bf[s][:, c0:c1, :].rearrange("p (c i) t -> p c t i", i=4)
            source = x_raw[s][:, :, c0:c1].rearrange("p t (c i) -> p c t i", i=4)
            if eng == "v":
                nc.vector.tensor_copy(dst, source)
            else:
                nc.scalar.activation(dst, source, ACT.Copy)

        def quant_x(s, c0, c1):
            nc.vector.quantize_mx(
                out=x_words[s][:, c0:c1].bitcast(FP8X4),
                scales=x_bytes[s][:, c0:c1],
                in_=x_bf[s][:, c0:c1, :].rearrange("p c t -> p (c t)"),
            )

        def tokens(s):
            cast("s", s, 0, 256)
            cast("s", s, 256, 384)
            cast("v", s, 384, 512)
            cast("s", s, 512, T)
            for c in CHUNKS:
                quant_x(s, *c)

        def gather_tiles(s, e, words_tag, bytes_tag):
            g_words[s, e] = keep.tile([P, C], U32, align_bytes=64, name="g_words%d_%d" % (s, e), tag=words_tag)
            g_bytes[s, e] = keep.tile([P, C], U8, align_bytes=64, name="g_bytes%d_%d" % (s, e), tag=bytes_tag)

        def gather(s, e, c0, c1):
            idx = offsets[:, (e * C + c0) // 16 : (e * C + c1) // 16]
            nc.vector.tensor_copy(g_words[s, e][:, c0:c1], x_words[s][:].indirect(idx))
            nc.vector.tensor_copy(g_bytes[s, e][:, c0:c1], x_bytes[s][:].indirect(idx))

        banks = {}

        def mm1(t, s):
            e, c0 = t // 2, (t % 2) * P
            for b in range(HP):
                if s == 0:
                    banks[t, b] = mmp.tile([P, 512], F32, name="acc")
                nc.tensor.matmul_mx(
                    out=banks[t, b][:],
                    lhsT=g_words[s, e][:, c0 : c0 + P].bitcast(FP8X4),
                    lhsT_scale=g_bytes[s, e][:, c0 : c0 + P],
                    rhs=w1_t[e][s][:, b * 1024 : (b + 1) * 1024].bitcast(FP4X4),
                    rhs_scale=w1_s[e][:, s * H + b * 512 : s * H + (b + 1) * 512],
                    start=(s == 0),
                    stop=(s == KP - 1),
                )

        def hidden(t, engs="ss"):
            for b in range(HP):
                nc.scalar.activation(
                    h_bf[t][:, b * 512 : (b + 1) * 512].rearrange("c (u p e) -> c u p e", u=2, e=2),
                    banks[t, b][:].rearrange("c (p u e) -> c u p e", u=2, e=2),
                    ACT.Gelu_apprx_tanh,
                )
                xt = xtp.tile([P, 2, P], F32, name="xt")
                pairs = h_bf[t][:].bitcast(F32)
                for u in range(2):
                    nc.tensor.transpose(xt[:, u, :], pairs[:, b * 256 + u * P : b * 256 + (u + 1) * P], ident[:])
                dst = h_gr[t][:, b].rearrange("p c t -> p (c t)").bitcast(F32).rearrange("p (c u) -> p c u", u=2)
                source = xt[:].rearrange("p u c -> p c u")
                if engs[b] == "s":
                    nc.scalar.copy(dst, source)
                else:
                    nc.vector.tensor_copy(dst, source)
            nc.vector.quantize_mx(
                out=h_words[t][:].bitcast(FP8X4),
                scales=h_bytes[t][:],
                in_=h_gr[t][:].rearrange("p b c t -> p (b c t)"),
            )

        def mm2(t):
            e = t // 2
            y = yp.tile([P, NB, P], F32, name="y")
            for m in range(NB):
                for b in range(HP):
                    w0 = b * N + m * P
                    nc.tensor.matmul_mx(
                        out=y[:, m, :],
                        lhsT=w2_t[e][:, 2 * w0 : 2 * (w0 + P)].bitcast(FP4X4),
                        lhsT_scale=w2_s[:, e * HP * N + w0 : e * HP * N + w0 + P],
                        rhs=h_words[t][:, b * P : (b + 1) * P].bitcast(FP8X4),
                        rhs_scale=h_bytes[t][:, b * P : (b + 1) * P],
                        start=(b == 0),
                        stop=(b == HP - 1),
                    )
            nc.scalar.copy(y_g[t][:], y[:])

        def scatter(t, m):
            idx = offsets[:, t * (P // 16) : (t + 1) * (P // 16)]
            nc.vector.tensor_tensor(win[m][:].indirect(idx), y_g[t][:, m, :], gate_t[:, m, t * P : (t + 1) * P], MULT)

        def finish(m):
            nc.vector.tensor_tensor(res[m][:], win[m][:], xr_t[m][:], mybir.AluOpType.add)
            nc.sync.dma_start(out[m * P : (m + 1) * P, :], res[m][:])

        for s in range(KP):
            gather_tiles(s, 0, "g_words%d_0" % s, "g_bytes%d_0" % s)
        gather_tiles(0, 1, "g_words0_1", "g_bytes0_1")
        gather_tiles(2, 1, "g_words2_1", "g_bytes2_1")
        tokens(0)
        gather(0, 0, 0, C)
        gather(0, 1, 0, C)
        tokens(1)
        gather(1, 0, 0, C)
        for t in range(2):
            mm1(t, 0)
            mm1(t, 1)
        tokens(2)
        for t in range(2):
            gather(2, 0, t * P, (t + 1) * P)
            mm1(t, 2)
        hidden(0, "sv")
        mm2(0)
        gather_tiles(1, 1, "x_bf2", "x_raw2")
        gather(1, 1, 0, C)
        gather(2, 1, 0, C)
        hidden(1)
        mm2(1)
        for s in range(KP):
            mm1(2, s)
        for m in range(NB):
            scatter(0, m)
        hidden(2)
        mm2(2)
        for s in range(KP):
            mm1(3, s)
        for m in range(NB):
            scatter(1, m)
        hidden(3)
        mm2(3)
        for m in range(NB):
            scatter(2, m)
        scatter(3, 0)
        scatter(3, 1)
        finish(0)
        scatter(3, 2)
        finish(1)
        finish(2)
